import numpy as np
import ml_dtypes


def mxq(x, axis, fmt="e4m3"):
    dtype, down = {"e4m3": (ml_dtypes.float8_e4m3fn, 7), "e5m2": (ml_dtypes.float8_e5m2, 14)}[fmt]
    v = np.moveaxis(np.asarray(x, np.float32).astype(ml_dtypes.bfloat16).astype(np.float64), axis, -1)
    blocks = v.reshape(v.shape[:-1] + (-1, 32))
    amax = np.abs(blocks).max(-1, keepdims=True)
    byte = np.maximum(np.where(amax > 0, np.frexp(amax)[1] - 1 + 127, 0) - down, 1)
    scale = np.exp2(byte - 127.0)
    codes = (blocks / scale).astype(np.float32).astype(dtype).astype(np.float64)
    return np.moveaxis((codes * scale).reshape(v.shape), -1, axis)


WIDE = False


def mx_kscale(k):
    if not WIDE:
        return np.ones(k)
    levels = np.array([10, -10, 5, -5, 0])
    if k % 512:
        return np.exp2(np.random.permutation(np.resize(levels, k // 32))).repeat(32)
    a = np.empty((k // 512, 16))
    for p in range(k // 512):
        a[p, :8] = np.random.permutation(np.resize(levels, 8))
        for g in range(8):
            far = levels[np.abs(levels - a[p, g]) >= 10]
            a[p, g + 8] = far[np.random.randint(len(far))]
    return np.exp2(a.ravel()).repeat(32)


BF16 = ml_dtypes.bfloat16


def bf(x):
    return np.asarray(x, np.float32).astype(BF16)


def f64(x):
    return np.asarray(x).astype(np.float64)


E2M1 = np.array([0.0, 0.5, 1.0, 1.5, 2.0, 3.0, 4.0, 6.0, -0.0, -0.5, -1.0, -1.5, -2.0, -3.0, -4.0, -6.0])


def pack_weight(w, fmt):
    k, n = w.shape
    w = f64(bf(w)).reshape(k // 32, 32, n)
    amax = np.abs(w).max(1)
    if fmt == "e4m3":
        byte = np.frexp(amax)[1] - 1 + 127 - 7
    else:
        mant, ex = np.frexp(amax / 6.0)
        byte = np.where(mant > 0.5, ex, ex - 1) + 127
    byte = np.clip(np.where(amax > 0, byte, 1), 1, 254)
    scaled = (w * np.exp2(127.0 - byte)[:, None, :]).reshape(k, n).astype(np.float32)
    by_word = np.ascontiguousarray(scaled.reshape(k // 512, 128, 4, n).transpose(0, 1, 3, 2))
    if fmt == "e4m3":
        words = by_word.astype(ml_dtypes.float8_e4m3fn).view(np.uint8)
    else:
        c = by_word.astype(ml_dtypes.float4_e2m1fn).view(np.uint8) & 0xF
        words = c[..., 0::2] | (c[..., 1::2] << 4)
    return np.ascontiguousarray(words), np.ascontiguousarray(byte.astype(np.uint8).reshape(k // 512, 16, n))


def unpack_weight(words, scales, fmt):
    g, p, n, _ = words.shape
    if fmt == "e4m3":
        vals = np.ascontiguousarray(words).view(ml_dtypes.float8_e4m3fn).astype(np.float64)
    else:
        nib = np.empty((g, p, n, 4), np.uint8)
        nib[..., 0::2] = words & 0xF
        nib[..., 1::2] = words >> 4
        vals = E2M1[nib]
    vals = vals * np.repeat(np.exp2(scales.astype(np.float64) - 127.0), 8, axis=1)[..., None]
    return vals.transpose(0, 1, 3, 2).reshape(g * 512, n)

def planes(Y):
    n, m = Y.shape
    b = f64(bf(Y)).reshape(n // 32, 32, m)
    amax = np.abs(b).max(1)
    byte = np.clip(np.where(amax > 0, np.frexp(amax)[1] - 1 + 127 - 7, 1), 1, 254)
    codes = (b * np.exp2(127.0 - byte)[:, None, :]).reshape(n, m).astype(np.float32).astype(ml_dtypes.float8_e4m3fn).view(np.uint8)
    words = codes.reshape(n // 512, 128, 4, m).transpose(0, 1, 3, 2)
    return np.ascontiguousarray(words), np.ascontiguousarray(byte.astype(np.uint8).reshape(n // 512, 16, m))


N, M, D, H = 1024, 1024, 512, 1024


def head_sensitivity(pre, v):
    act = np.tanh(pre)
    return (1.0 - act * act) * v[None, :]


def setup_inputs():
    s, t = mx_kscale(D), mx_kscale(H)
    x = bf(np.random.standard_normal((N, D)) * s[None, :])
    z = bf(np.random.standard_normal((M, D)) * s[None, :])
    w_words, w_scales = pack_weight(np.random.standard_normal((D, H)) / np.sqrt(D) / s[:, None], "e4m3")
    return {
        "x": x,
        "z": z,
        "w_words": w_words,
        "w_scales": w_scales,
        "lam": bf((1.0 + 0.1 * np.random.standard_normal(D)) / (s * s)),
        "v1": bf(np.random.standard_normal(H) * t),
        "v2": bf(np.random.standard_normal(H) / t),
    }


def core(x, z, w_words, w_scales, lam, v1, v2):
    x64 = f64(x)
    xq = mxq(x64, 1, "e4m3")
    zq = mxq(f64(z), 1, "e4m3")
    wq = unpack_weight(w_words, w_scales, "e4m3")
    a = head_sensitivity(xq @ wq, f64(v1))
    b = head_sensitivity(zq @ wq, f64(v2))
    t = (mxq(a, 1, "e4m3") @ mxq(b, 1, "e4m3").T) / np.sqrt(H)
    xl = mxq(x64 * f64(lam)[None, :], 1, "e4m3")
    q = (xl @ zq.T) / np.sqrt(D) + 1.0
    return q * t


def reference(x, z, w_words, w_scales, lam, v1, v2):
    R_out = core(x, z, w_words, w_scales, lam, v1, v2)
    words, scales = planes(R_out.T)
    return R_out, words, scales

@@ -1,0 +1,368 @@
+import math
+from contextlib import ExitStack
+
+import concourse.mybir as mybir
+from concourse.masks import make_identity
+
+N, M, D, H = 1024, 1024, 512, 1024
+FLOPS = 2 * (N * H * D + M * H * D + N * M * H + N * M * D)
+
+F32 = mybir.dt.float32
+BF16 = mybir.dt.bfloat16
+I32 = mybir.dt.int32
+U8 = mybir.dt.uint8
+FP8X4 = mybir.dt.float8_e4m3fn_x4
+ACT = mybir.ActivationFunctionType
+ALU = mybir.AluOpType
+
+P = 128
+HALF = 512
+HALVES = 2
+T4 = 4
+
+DVE_U = (0,)
+
+
+def tile_crossheadtangentkernellinearisedlaplace_x2_kernel(
+    tc, x, z, w_words, w_scales, lam, v1, v2, out_0, out_1, out_2
+):
+    nc = tc.nc
+    with ExitStack() as ctx:
+        keep = ctx.enter_context(tc.tile_pool(name="keep", bufs=1))
+        work = ctx.enter_context(tc.tile_pool(name="work", bufs=3))
+        psum = ctx.enter_context(tc.psum_pool(name="psum", bufs=2))
+        ctx.enter_context(tc.manual_schedule())
+
+        ws_raw = keep.tile([P, H], U8, align_bytes=64, name="ws_raw")
+        nc.vector.memset(ws_raw[:].bitcast(I32), 0)
+        warm = keep.tile([P, 1], F32, name="warm")
+        nc.vector.memset(warm[:], 0.0)
+        warm_out = keep.tile([P, 1], F32, name="warm_out")
+        ident = keep.tile([P, P], F32, name="ident")
+        make_identity(nc, ident[:])
+
+        rows = {}
+        src = {"x": x, "z": z}
+
+        def load_rows(which, hf, j0, nj):
+            if (which, hf) not in rows:
+                rows[which, hf] = keep.tile([P, 4, D], BF16, align_bytes=64, name="rows_%s%d" % (which, hf))
+            nc.sync.dma_start(
+                out=rows[which, hf][:, j0 : j0 + nj, :],
+                in_=src[which][HALF * hf + P * j0 : HALF * hf + P * (j0 + nj), :].rearrange("(j p) k -> p j k", p=P),
+            )
+
+        load_rows("z", 0, 0, 2)
+        load_rows("z", 0, 2, 2)
+        w_raw = keep.tile([P, H], I32, align_bytes=64, name="w_raw")
+        w_dram = w_words[0].rearrange("p n t -> p (n t)")
+
+        def load_w(g):
+            nc.sync.dma_start(
+                out=w_raw[:, HALF * g : HALF * (g + 1)],
+                in_=w_dram[:, 4 * HALF * g : 4 * HALF * (g + 1)].bitcast(I32),
+            )
+
+        load_w(0)
+        load_w(1)
+        load_rows("x", 0, 0, 4)
+        load_rows("z", 1, 0, 4)
+        load_rows("x", 1, 0, 4)
+
+        for q in range(4):
+            nc.scalar.dma_start(
+                out=ws_raw[32 * q : 32 * q + 4, :].bitcast(I32),
+                in_=w_scales[0, 4 * q : 4 * q + 4, :].bitcast(I32),
+            )
+        nc.scalar.activation(warm_out[:], warm[:], ACT.Sigmoid)
+
+        v_raw = [keep.tile([P, 2, T4], BF16, name="v_raw%d" % o) for o in range(2)]
+        lam_sb = keep.tile([P, T4], BF16, name="lam_sb")
+        nc.gpsimd.dma_start(out=v_raw[1][:], in_=v2.rearrange("(g p t) -> p g t", p=P, t=T4))
+        nc.gpsimd.dma_start(out=v_raw[0][:], in_=v1.rearrange("(g p t) -> p g t", p=P, t=T4))
+        nc.gpsimd.dma_start(out=lam_sb[:], in_=lam.rearrange("(p t) -> p t", t=T4))
+        v_pos = keep.tile([P, 2, 2, T4], F32, name="v_pos")
+        v_neg = keep.tile([P, 2, 2, T4], F32, name="v_neg")
+
+        def v_scale(o):
+            nc.vector.tensor_scalar(out=v_pos[:, o], in0=v_raw[o][:], scalar1=4.0, scalar2=None, op0=ALU.mult)
+            nc.vector.tensor_scalar(out=v_neg[:, o], in0=v_raw[o][:], scalar1=-4.0, scalar2=None, op0=ALU.mult)
+
+        grouped = {}
+        bank = {}
+
+        def prep_tr(which, hf, b):
+            t = psum.tile([P, 2, 2, P], F32, tag="tr", bufs=2, name="tr")
+            bank[which, hf, b] = t
+            for jj in range(2):
+                words = rows[which, hf][:, 2 * b + jj, :].bitcast(F32)
+                for u in range(2):
+                    nc.tensor.transpose(t[:, jj, u, :], words[:, u::2], ident[:])
+
+        def prep_evac(which, hf, b, eng):
+            if (which, hf) not in grouped:
+                grouped[which, hf] = keep.tile([P, HALF, T4], BF16, align_bytes=64, name="grouped_%s%d" % (which, hf))
+            dst = (
+                grouped[which, hf][:, 256 * b : 256 * (b + 1), :]
+                .rearrange("p n t -> p (n t)")
+                .bitcast(F32)
+                .rearrange("p (j r u) -> p j r u", j=2, u=2)
+            )
+            s = bank[which, hf, b][:].rearrange("p j u r -> p j r u")
+            if eng == "v":
+                nc.vector.tensor_copy(out=dst, in_=s)
+            else:
+                nc.scalar.copy(out=dst, in_=s)
+
+        codes = {}
+        scales = {}
+
+        def quantize(key, tile3, pool=keep):
+            name = "_".join(str(k) for k in key)
+            codes[key] = pool.tile([P, HALF], I32, align_bytes=64, name="codes_" + name)
+            scales[key] = pool.tile([P, HALF], U8, align_bytes=64, name="scales_" + name)
+            nc.vector.quantize_mx(
+                out=codes[key][:].bitcast(FP8X4),
+                scales=scales[key][:],
+                in_=tile3[:].rearrange("p n t -> p (n t)"),
+            )
+
+        def prep_q(which, hf):
+            quantize((which, hf), grouped[which, hf])
+
+        xl = {}
+
+        def lam_mul(hf):
+            xl[hf] = keep.tile([P, HALF, T4], BF16, align_bytes=64, name="xl%d" % hf)
+            nc.vector.tensor_tensor(
+                out=xl[hf][:],
+                in0=grouped["x", hf][:],
+                in1=lam_sb[:].unsqueeze(1).to_broadcast([P, HALF, T4]),
+                op=ALU.mult,
+            )
+
+        def lam_q(hf):
+            quantize(("l", hf), xl[hf])
+
+        w_codes = keep.tile([P, H], I32, align_bytes=64, name="w_codes")
+        w_sc = keep.tile([P, H], U8, align_bytes=64, name="w_sc")
+
+        def w_perm(g):
+            cols = slice(HALF * g, HALF * (g + 1))
+            for dst, s in ((w_codes, w_raw), (w_sc, ws_raw)):
+                nc.vector.tensor_copy(
+                    out=dst[:, cols].rearrange("p (t m) -> p t m", t=T4),
+                    in_=s[:, cols].rearrange("p (m t) -> p t m", t=T4),
+                )
+
+        units = [("z", 0, 0), ("z", 0, 1), ("x", 0, 0), ("x", 0, 1), ("z", 1, 0), ("z", 1, 1), ("x", 1, 0), ("x", 1, 1)]
+        sig = {}
+        comp = {}
+        abf = {}
+
+        def h_mm(k, t):
+            which, hf, g = units[k]
+            acc = psum.tile([P, HALF], F32, tag="acc", bufs=4, name="acc")
+            c0 = HALF * g + P * t
+            nc.tensor.matmul_mx(
+                out=acc[:],
+                lhsT=w_codes[:, c0 : c0 + P].bitcast(FP8X4),
+                lhsT_scale=w_sc[:, c0 : c0 + P],
+                rhs=codes[which, hf][:].bitcast(FP8X4),
+                rhs_scale=scales[which, hf][:],
+                start=True,
+                stop=True,
+            )
+            if t == 0:
+                sig[k] = work.tile([P, T4, HALF], F32, align_bytes=64, name="sig")
+                comp[k] = work.tile([P, T4, HALF], F32, align_bytes=64, name="comp")
+            nc.scalar.activation(sig[k][:, t, :], acc[:], ACT.Sigmoid, scale=2.0)
+
+        def h_comp(k, t):
+            which, hf, g = units[k]
+            o = 0 if which == "x" else 1
+            neg = v_neg[:, o, g, t : t + 1]
+            pos = v_pos[:, o, g, t : t + 1]
+            if t in DVE_U:
+                nc.vector.tensor_scalar(
+                    out=comp[k][:, t, :], in0=sig[k][:, t, :], scalar1=neg, scalar2=pos, op0=ALU.mult, op1=ALU.add
+                )
+            else:
+                nc.scalar.activation(comp[k][:, t, :], sig[k][:, t, :], ACT.Identity, bias=pos, scale=neg)
+
+        def h_prod(k, part):
+            if part == 0:
+                abf[k] = work.tile([P, HALF, T4], BF16, align_bytes=64, name="abf")
+            cols = slice(256 * part, 256 * (part + 1))
+            nc.vector.tensor_tensor(
+                out=abf[k][:, cols, :].rearrange("p (c i) t -> p c t i", i=4),
+                in0=sig[k][:, :, cols].rearrange("p t (c i) -> p c t i", i=4),
+                in1=comp[k][:, :, cols].rearrange("p t (c i) -> p c t i", i=4),
+                op=ALU.mult,
+            )
+
+        def h_q(k):
+            which, hf, g = units[k]
+            quantize(("h" + which, hf, g), abf[k])
+
+        q_sb = {}
+        t_ps = {}
+        res = {}
+        res16 = {}
+        pbank = {}
+        pgr = {}
+
+        def f_mm(f):
+            hf, g, i = f
+            cols = slice(P * i, P * (i + 1))
+            qa = psum.tile([P, HALF], F32, tag="acc", bufs=4, name="acc")
+            nc.tensor.matmul_mx(
+                out=qa[:],
+                lhsT=codes["l", hf][:, cols].bitcast(FP8X4),
+                lhsT_scale=scales["l", hf][:, cols],
+                rhs=codes["z", g][:].bitcast(FP8X4),
+                rhs_scale=scales["z", g][:],
+                start=True,
+                stop=True,
+            )
+            ta = psum.tile([P, HALF], F32, tag="tt", bufs=2, name="ta")
+            for kk in range(2):
+                nc.tensor.matmul_mx(
+                    out=ta[:],
+                    lhsT=codes["hx", hf, kk][:, cols].bitcast(FP8X4),
+                    lhsT_scale=scales["hx", hf, kk][:, cols],
+                    rhs=codes["hz", g, kk][:].bitcast(FP8X4),
+                    rhs_scale=scales["hz", g, kk][:],
+                    start=(kk == 0),
+                    stop=(kk == 1),
+                )
+            t_ps[f] = ta
+            q_sb[f] = work.tile([P, HALF], F32, align_bytes=64, name="q_sb")
+            nc.scalar.activation(q_sb[f][:], qa[:], ACT.Copy, scale=1.0 / math.sqrt(D), bias=1.0)
+
+        def f_res(f):
+            hf, g, i = f
+            res[f] = work.tile([P, HALF], F32, align_bytes=64, name="res", bufs=4)
+            nc.vector.scalar_tensor_tensor(
+                out=res[f][:], in0=t_ps[f][:], scalar=1.0 / math.sqrt(H), in1=q_sb[f][:], op0=ALU.mult, op1=ALU.mult
+            )
+            r0 = HALF * hf + P * i
+            nc.sync.dma_start(out=out_0[r0 : r0 + P, HALF * g : HALF * (g + 1)], in_=res[f][:])
+
+        def f_cast(f):
+            res16[f] = work.tile([P, HALF], BF16, align_bytes=64, name="res16")
+            nc.vector.tensor_copy(out=res16[f][:], in_=res[f][:])
+
+        def f_tr(f):
+            hf, g, i = f
+            if i % 2 == 0:
+                pbank[hf, g, i // 2] = psum.tile([P, 2, 2, P], F32, tag="tr", bufs=2, name="tr")
+            words = res16[f][:].bitcast(F32)
+            for u in range(2):
+                nc.tensor.transpose(pbank[hf, g, i // 2][:, i % 2, u, :], words[:, u::2], ident[:])
+
+        def f_evac(f):
+            hf, g, i = f
+            b = i // 2
+            if b == 0:
+                pgr[hf, g] = work.tile([P, HALF, T4], BF16, align_bytes=64, name="pgr", bufs=2)
+            dst = (
+                pgr[hf, g][:, 256 * b : 256 * (b + 1), :]
+                .rearrange("p n t -> p (n t)")
+                .bitcast(F32)
+                .rearrange("p (j r u) -> p j r u", j=2, u=2)
+            )
+            nc.scalar.copy(out=dst, in_=pbank[hf, g, b][:].rearrange("p j u r -> p j r u"))
+
+        def f_q(f):
+            hf, g, i = f
+            b = i // 2
+            key = ("p", hf, g)
+            if b == 0:
+                codes[key] = keep.tile([P, HALF], I32, align_bytes=64, name="codes_p%d%d" % (hf, g))
+                scales[key] = keep.tile([P, HALF], U8, align_bytes=64, name="scales_p%d%d" % (hf, g))
+            cols = slice(256 * b, 256 * (b + 1))
+            nc.vector.quantize_mx(
+                out=codes[key][:, cols].bitcast(FP8X4),
+                scales=scales[key][:, cols],
+                in_=pgr[hf, g][:, cols, :].rearrange("p n t -> p (n t)"),
+            )
+            c0 = HALF * hf + 256 * b
+            nc.sync.dma_start(
+                out=out_1[g].rearrange("p n t -> p (n t)")[:, 4 * c0 : 4 * (c0 + 256)].bitcast(I32),
+                in_=codes[key][:, cols],
+            )
+            if b == 1:
+                for q in range(4):
+                    nc.sync.dma_start(
+                        out=out_2[g, 4 * q : 4 * q + 4, HALF * hf : HALF * (hf + 1)].bitcast(I32),
+                        in_=scales[key][32 * q : 32 * q + 4, :].bitcast(I32),
+                    )
+
+        prep_tr("z", 0, 0)
+        prep_tr("z", 0, 1)
+        w_perm(0)
+        prep_evac("z", 0, 0, "s")
+        prep_evac("z", 0, 1, "v")
+        v_scale(1)
+        prep_q("z", 0)
+
+        finals = [(hf, g, i) for hf in range(2) for g in range(2) for i in range(4)]
+        items = []
+        nf = 0
+        for k in range(8):
+            for t in range(T4):
+                items.append(("h", k, t))
+                if k >= 6 and t % 2 == 0:
+                    items.append(("f",) + finals[nf])
+                    nf += 1
+        items.extend(("f",) + f for f in finals[nf:])
+
+        hooks = {
+            1: [lambda: w_perm(1), lambda: v_scale(0)],
+            3: [lambda: prep_tr("x", 0, 0)],
+            4: [lambda: prep_evac("x", 0, 0, "v"), lambda: prep_tr("x", 0, 1)],
+            5: [lambda: prep_evac("x", 0, 1, "v")],
+            6: [lambda: prep_q("x", 0)],
+            8: [lambda: lam_mul(0)],
+            9: [lambda: lam_q(0)],
+            10: [lambda: prep_tr("z", 1, 0)],
+            11: [lambda: prep_evac("z", 1, 0, "v"), lambda: prep_tr("z", 1, 1)],
+            12: [lambda: prep_evac("z", 1, 1, "v")],
+            13: [lambda: prep_q("z", 1)],
+            17: [lambda: prep_tr("x", 1, 0)],
+            18: [lambda: prep_evac("x", 1, 0, "v"), lambda: prep_tr("x", 1, 1)],
+            19: [lambda: prep_evac("x", 1, 1, "v")],
+            20: [lambda: prep_q("x", 1)],
+            24: [lambda: lam_mul(1)],
+            26: [lambda: lam_q(1)],
+        }
+
+        def at(s, kind):
+            return 0 <= s < len(items) and items[s][0] == kind
+
+        for s in range(len(items) + 7):
+            if at(s, "h"):
+                h_mm(items[s][1], items[s][2])
+            if at(s, "f"):
+                f_mm(items[s][1:])
+            if at(s - 1, "f"):
+                f_res(items[s - 1][1:])
+            if at(s - 1, "h"):
+                h_comp(items[s - 1][1], items[s - 1][2])
+            if at(s - 2, "h") and items[s - 2][2] == 3:
+                h_prod(items[s - 2][1], 0)
+            if at(s - 2, "f"):
+                f_cast(items[s - 2][1:])
+            if at(s - 3, "h") and items[s - 3][2] == 3:
+                h_prod(items[s - 3][1], 1)
+            if at(s - 3, "f"):
+                f_tr(items[s - 3][1:])
+            if at(s - 4, "f") and items[s - 4][3] % 2 == 1:
+                f_evac(items[s - 4][1:])
+            for hook in hooks.get(s, []):
+                hook()
+            if at(s - 4, "h") and items[s - 4][2] == 3:
+                h_q(items[s - 4][1])
+            if at(s - 5, "f") and items[s - 5][3] % 2 == 1:
+                f_q(items[s - 5][1:])

@@ -20,7 +20,30 @@ HALF = 512
 HALVES = 2
 T4 = 4
 
-DVE_U = (0,)
+DVE_U = ((0, 1, 2, 3,), (0,), (0,), (0,), (0,), (0,), (0, 1, 2,), (0, 1, 2,))
+EVAC = {("z", 0, 0): "s", ("z", 0, 1): "s", ("x", 0, 0): "s", ("x", 0, 1): "v",
+        ("z", 1, 0): "s", ("z", 1, 1): "v", ("x", 1, 0): "s", ("x", 1, 1): "s"}
+FDVE = ((1,0,1), (1,1,1),)
+CAST_ACT = ((0,0,3), (0,1,1), (0,1,3), (1,0,1), (1,0,3), (1,1,1), (1,1,3),)
+EARLY_F = ((5,1), (5,2), (5,3),)
+EARLY_Q = ((4,2), (5,2), (6,2), (7,1), (7,3),)
+HOOKS = {
+    (0, 0, 0): ["w 1"],
+    (0, 0, 1): ["tr x 0 0"],
+    (0, 1, 1): ["ev x 0 0", "tr x 0 1"],
+    (0, 2, 1): ["ev x 0 1"],
+    (1, 1, 0): ["q x 0", "v 0", "tr z 1 0"],
+    (1, 2, 0): ["ev z 1 0", "tr z 1 1"],
+    (1, 3, 0): ["ev z 1 1"],
+    (2, 0, 0): ["lm 0"],
+    (2, 1, 0): ["q z 1", "tr x 1 0"],
+    (2, 2, 0): ["ev x 1 0", "tr x 1 1"],
+    (2, 3, 0): ["lq 0"],
+    (3, 0, 0): ["ev x 1 1"],
+    (3, 1, 0): ["q x 1"],
+    (3, 2, 0): ["lm 1"],
+    (3, 3, 0): ["lq 1"],
+}
 
 
 def tile_crossheadtangentkernellinearisedlaplace_x2_kernel(
@@ -33,11 +56,14 @@ def tile_crossheadtangentkernellinearisedlaplace_x2_kernel(
         psum = ctx.enter_context(tc.psum_pool(name="psum", bufs=2))
         ctx.enter_context(tc.manual_schedule())
 
-        ws_raw = keep.tile([P, H], U8, align_bytes=64, name="ws_raw")
-        nc.vector.memset(ws_raw[:].bitcast(I32), 0)
         warm = keep.tile([P, 1], F32, name="warm")
         nc.vector.memset(warm[:], 0.0)
         warm_out = keep.tile([P, 1], F32, name="warm_out")
+        nc.scalar.activation(warm_out[:], warm[:], ACT.Sigmoid)
+        ws_raw = keep.tile([P, H], U8, align_bytes=64, name="ws_raw")
+        nc.vector.memset(ws_raw[:].bitcast(I32), 0)
+        v_raw = [keep.tile([P, 2, T4], BF16, name="v_raw%d" % o) for o in range(2)]
+        lam_sb = keep.tile([P, T4], BF16, name="lam_sb")
         ident = keep.tile([P, P], F32, name="ident")
         make_identity(nc, ident[:])
 
@@ -53,7 +79,6 @@ def tile_crossheadtangentkernellinearisedlaplace_x2_kernel(
             )
 
         load_rows("z", 0, 0, 2)
-        load_rows("z", 0, 2, 2)
         w_raw = keep.tile([P, H], I32, align_bytes=64, name="w_raw")
         w_dram = w_words[0].rearrange("p n t -> p (n t)")
 
@@ -63,24 +88,22 @@ def tile_crossheadtangentkernellinearisedlaplace_x2_kernel(
                 in_=w_dram[:, 4 * HALF * g : 4 * HALF * (g + 1)].bitcast(I32),
             )
 
-        load_w(0)
-        load_w(1)
-        load_rows("x", 0, 0, 4)
-        load_rows("z", 1, 0, 4)
-        load_rows("x", 1, 0, 4)
-
         for q in range(4):
-            nc.scalar.dma_start(
+            nc.sync.dma_start(
                 out=ws_raw[32 * q : 32 * q + 4, :].bitcast(I32),
                 in_=w_scales[0, 4 * q : 4 * q + 4, :].bitcast(I32),
             )
-        nc.scalar.activation(warm_out[:], warm[:], ACT.Sigmoid)
+        load_w(0)
+        load_rows("z", 0, 2, 2)
+        nc.sync.dma_start(out=v_raw[1][:], in_=v2.rearrange("(g p t) -> p g t", p=P, t=T4))
+        load_w(1)
+        load_rows("x", 0, 0, 4)
+        nc.sync.dma_start(out=v_raw[0][:], in_=v1.rearrange("(g p t) -> p g t", p=P, t=T4))
+        nc.sync.dma_start(out=lam_sb[:], in_=lam.rearrange("(p t) -> p t", t=T4))
+        load_rows("z", 1, 0, 4)
+        load_rows("x", 1, 0, 4)
 
-        v_raw = [keep.tile([P, 2, T4], BF16, name="v_raw%d" % o) for o in range(2)]
-        lam_sb = keep.tile([P, T4], BF16, name="lam_sb")
-        nc.gpsimd.dma_start(out=v_raw[1][:], in_=v2.rearrange("(g p t) -> p g t", p=P, t=T4))
-        nc.gpsimd.dma_start(out=v_raw[0][:], in_=v1.rearrange("(g p t) -> p g t", p=P, t=T4))
-        nc.gpsimd.dma_start(out=lam_sb[:], in_=lam.rearrange("(p t) -> p t", t=T4))
+
         v_pos = keep.tile([P, 2, 2, T4], F32, name="v_pos")
         v_neg = keep.tile([P, 2, 2, T4], F32, name="v_neg")
 
@@ -127,8 +150,20 @@ def tile_crossheadtangentkernellinearisedlaplace_x2_kernel(
                 in_=tile3[:].rearrange("p n t -> p (n t)"),
             )
 
-        def prep_q(which, hf):
-            quantize((which, hf), grouped[which, hf])
+        def prep_q(which, hf, b=None):
+            if b is None:
+                quantize((which, hf), grouped[which, hf])
+                return
+            key = (which, hf)
+            if b == 0:
+                codes[key] = keep.tile([P, HALF], I32, align_bytes=64, name="codes_%s%d" % key)
+                scales[key] = keep.tile([P, HALF], U8, align_bytes=64, name="scales_%s%d" % key)
+            cols = slice(256 * b, 256 * (b + 1))
+            nc.vector.quantize_mx(
+                out=codes[key][:, cols].bitcast(FP8X4),
+                scales=scales[key][:, cols],
+                in_=grouped[key][:, cols, :].rearrange("p n t -> p (n t)"),
+            )
 
         xl = {}
 
@@ -160,30 +195,30 @@ def tile_crossheadtangentkernellinearisedlaplace_x2_kernel(
         comp = {}
         abf = {}
 
-        def h_mm(k, t):
+        def h_mm(k, t, c0, c1):
             which, hf, g = units[k]
             acc = psum.tile([P, HALF], F32, tag="acc", bufs=4, name="acc")
-            c0 = HALF * g + P * t
+            if t == 0 and c0 == 0:
+                sig[k] = work.tile([P, T4, HALF], F32, align_bytes=64, name="sig")
+                comp[k] = work.tile([P, T4, HALF], F32, align_bytes=64, name="comp")
+            h0 = HALF * g + P * t
             nc.tensor.matmul_mx(
-                out=acc[:],
-                lhsT=w_codes[:, c0 : c0 + P].bitcast(FP8X4),
-                lhsT_scale=w_sc[:, c0 : c0 + P],
-                rhs=codes[which, hf][:].bitcast(FP8X4),
-                rhs_scale=scales[which, hf][:],
+                out=acc[:, : c1 - c0],
+                lhsT=w_codes[:, h0 : h0 + P].bitcast(FP8X4),
+                lhsT_scale=w_sc[:, h0 : h0 + P],
+                rhs=codes[which, hf][:, c0:c1].bitcast(FP8X4),
+                rhs_scale=scales[which, hf][:, c0:c1],
                 start=True,
                 stop=True,
             )
-            if t == 0:
-                sig[k] = work.tile([P, T4, HALF], F32, align_bytes=64, name="sig")
-                comp[k] = work.tile([P, T4, HALF], F32, align_bytes=64, name="comp")
-            nc.scalar.activation(sig[k][:, t, :], acc[:], ACT.Sigmoid, scale=2.0)
+            nc.scalar.activation(sig[k][:, t, c0:c1], acc[:, : c1 - c0], ACT.Sigmoid, scale=2.0)
 
         def h_comp(k, t):
             which, hf, g = units[k]
             o = 0 if which == "x" else 1
             neg = v_neg[:, o, g, t : t + 1]
             pos = v_pos[:, o, g, t : t + 1]
-            if t in DVE_U:
+            if t in DVE_U[k]:
                 nc.vector.tensor_scalar(
                     out=comp[k][:, t, :], in0=sig[k][:, t, :], scalar1=neg, scalar2=pos, op0=ALU.mult, op1=ALU.add
                 )
@@ -212,7 +247,7 @@ def tile_crossheadtangentkernellinearisedlaplace_x2_kernel(
         pbank = {}
         pgr = {}
 
-        def f_mm(f):
+        def f_qmm(f):
             hf, g, i = f
             cols = slice(P * i, P * (i + 1))
             qa = psum.tile([P, HALF], F32, tag="acc", bufs=4, name="acc")
@@ -225,6 +260,12 @@ def tile_crossheadtangentkernellinearisedlaplace_x2_kernel(
                 start=True,
                 stop=True,
             )
+            q_sb[f] = work.tile([P, HALF], F32, align_bytes=64, name="q_sb", bufs=12)
+            nc.scalar.activation(q_sb[f][:], qa[:], ACT.Copy, scale=1.0 / math.sqrt(D), bias=1.0)
+
+        def f_mm(f):
+            hf, g, i = f
+            cols = slice(P * i, P * (i + 1))
             ta = psum.tile([P, HALF], F32, tag="tt", bufs=2, name="ta")
             for kk in range(2):
                 nc.tensor.matmul_mx(
@@ -237,8 +278,6 @@ def tile_crossheadtangentkernellinearisedlaplace_x2_kernel(
                     stop=(kk == 1),
                 )
             t_ps[f] = ta
-            q_sb[f] = work.tile([P, HALF], F32, align_bytes=64, name="q_sb")
-            nc.scalar.activation(q_sb[f][:], qa[:], ACT.Copy, scale=1.0 / math.sqrt(D), bias=1.0)
 
         def f_res(f):
             hf, g, i = f
@@ -250,16 +289,22 @@ def tile_crossheadtangentkernellinearisedlaplace_x2_kernel(
             nc.sync.dma_start(out=out_0[r0 : r0 + P, HALF * g : HALF * (g + 1)], in_=res[f][:])
 
         def f_cast(f):
-            res16[f] = work.tile([P, HALF], BF16, align_bytes=64, name="res16")
-            nc.vector.tensor_copy(out=res16[f][:], in_=res[f][:])
+            res16[f] = work.tile([P, HALF], BF16, align_bytes=64, name="res16", bufs=4)
+            dst = res16[f][:].rearrange("p (u q e) -> p u q e", u=2, e=2)
+            s = res[f][:].rearrange("p (q u e) -> p u q e", u=2, e=2)
+            if f in CAST_ACT:
+                nc.scalar.copy(out=dst, in_=s)
+            else:
+                nc.vector.tensor_copy(out=dst, in_=s)
 
         def f_tr(f):
             hf, g, i = f
-            if i % 2 == 0:
-                pbank[hf, g, i // 2] = psum.tile([P, 2, 2, P], F32, tag="tr", bufs=2, name="tr")
-            words = res16[f][:].bitcast(F32)
-            for u in range(2):
-                nc.tensor.transpose(pbank[hf, g, i // 2][:, i % 2, u, :], words[:, u::2], ident[:])
+            bk = psum.tile([P, 2, 2, P], F32, tag="tr", bufs=2, name="tr")
+            pbank[hf, g, i // 2] = bk
+            for jj in range(2):
+                words = res16[hf, g, i - 1 + jj][:].bitcast(F32)
+                for u in range(2):
+                    nc.tensor.transpose(bk[:, jj, u, :], words[:, P * u : P * (u + 1)], ident[:])
 
         def f_evac(f):
             hf, g, i = f
@@ -272,7 +317,11 @@ def tile_crossheadtangentkernellinearisedlaplace_x2_kernel(
                 .bitcast(F32)
                 .rearrange("p (j r u) -> p j r u", j=2, u=2)
             )
-            nc.scalar.copy(out=dst, in_=pbank[hf, g, b][:].rearrange("p j u r -> p j r u"))
+            s = pbank[hf, g, b][:].rearrange("p j u r -> p j r u")
+            if f in FDVE:
+                nc.vector.tensor_copy(out=dst, in_=s)
+            else:
+                nc.scalar.copy(out=dst, in_=s)
 
         def f_q(f):
             hf, g, i = f
@@ -299,70 +348,106 @@ def tile_crossheadtangentkernellinearisedlaplace_x2_kernel(
                         in_=scales[key][32 * q : 32 * q + 4, :].bitcast(I32),
                     )
 
+        def hook(text):
+            w = text.split(" ")
+            a = [int(c) if c in ("0", "1") else c for c in w[1:]]
+            if w[0] == "tr":
+                prep_tr(a[0], a[1], a[2])
+            if w[0] == "ev":
+                prep_evac(a[0], a[1], a[2], EVAC[a[0], a[1], a[2]])
+            if w[0] == "q":
+                prep_q(a[0], a[1])
+            if w[0] == "lm":
+                lam_mul(a[0])
+            if w[0] == "lq":
+                lam_q(a[0])
+            if w[0] == "w":
+                w_perm(a[0])
+            if w[0] == "v":
+                v_scale(a[0])
+
         prep_tr("z", 0, 0)
         prep_tr("z", 0, 1)
         w_perm(0)
-        prep_evac("z", 0, 0, "s")
-        prep_evac("z", 0, 1, "v")
+        prep_evac("z", 0, 0, EVAC["z", 0, 0])
+        prep_q("z", 0, 0)
+        prep_evac("z", 0, 1, EVAC["z", 0, 1])
+        prep_q("z", 0, 1)
         v_scale(1)
-        prep_q("z", 0)
 
         finals = [(hf, g, i) for hf in range(2) for g in range(2) for i in range(4)]
         items = []
         nf = 0
+        nq = 8
         for k in range(8):
-            for t in range(T4):
-                items.append(("h", k, t))
-                if k >= 6 and t % 2 == 0:
-                    items.append(("f",) + finals[nf])
-                    nf += 1
-        items.extend(("f",) + f for f in finals[nf:])
+            for part in range(2 if k == 0 else 1):
+                for t in range(T4):
+                    if k == 0:
+                        items.append(("h", k, t, 256 * part, 256 * (part + 1)))
+                    else:
+                        items.append(("h", k, t, 0, HALF))
+                    if (k, t) in EARLY_F:
+                        items.append(("q",) + finals[nf])
+                        items.append(("f",) + finals[nf])
+                        nf += 1
+                    if (k, t) in EARLY_Q:
+                        items.append(("q",) + finals[nq])
+                        nq += 1
+        for n in range(nf, 16):
+            if n < 8 or n >= nq:
+                items.append(("q",) + finals[n])
+            items.append(("f",) + finals[n])
 
-        hooks = {
-            1: [lambda: w_perm(1), lambda: v_scale(0)],
-            3: [lambda: prep_tr("x", 0, 0)],
-            4: [lambda: prep_evac("x", 0, 0, "v"), lambda: prep_tr("x", 0, 1)],
-            5: [lambda: prep_evac("x", 0, 1, "v")],
-            6: [lambda: prep_q("x", 0)],
-            8: [lambda: lam_mul(0)],
-            9: [lambda: lam_q(0)],
-            10: [lambda: prep_tr("z", 1, 0)],
-            11: [lambda: prep_evac("z", 1, 0, "v"), lambda: prep_tr("z", 1, 1)],
-            12: [lambda: prep_evac("z", 1, 1, "v")],
-            13: [lambda: prep_q("z", 1)],
-            17: [lambda: prep_tr("x", 1, 0)],
-            18: [lambda: prep_evac("x", 1, 0, "v"), lambda: prep_tr("x", 1, 1)],
-            19: [lambda: prep_evac("x", 1, 1, "v")],
-            20: [lambda: prep_q("x", 1)],
-            24: [lambda: lam_mul(1)],
-            26: [lambda: lam_q(1)],
-        }
+        slots = []
+        cur = []
+        for it in items:
+            cur.append(it)
+            if it[0] != "q":
+                slots.append(cur)
+                cur = []
+        assert not cur
 
-        def at(s, kind):
-            return 0 <= s < len(items) and items[s][0] == kind
+        def main(s):
+            if 0 <= s < len(slots):
+                return slots[s][-1]
+            return ("none",)
 
-        for s in range(len(items) + 7):
-            if at(s, "h"):
-                h_mm(items[s][1], items[s][2])
-            if at(s, "f"):
-                f_mm(items[s][1:])
-            if at(s - 1, "f"):
-                f_res(items[s - 1][1:])
-            if at(s - 1, "h"):
-                h_comp(items[s - 1][1], items[s - 1][2])
-            if at(s - 2, "h") and items[s - 2][2] == 3:
-                h_prod(items[s - 2][1], 0)
-            if at(s - 2, "f"):
-                f_cast(items[s - 2][1:])
-            if at(s - 3, "h") and items[s - 3][2] == 3:
-                h_prod(items[s - 3][1], 1)
-            if at(s - 3, "f"):
-                f_tr(items[s - 3][1:])
-            if at(s - 4, "f") and items[s - 4][3] % 2 == 1:
-                f_evac(items[s - 4][1:])
-            for hook in hooks.get(s, []):
-                hook()
-            if at(s - 4, "h") and items[s - 4][2] == 3:
-                h_q(items[s - 4][1])
-            if at(s - 5, "f") and items[s - 5][3] % 2 == 1:
-                f_q(items[s - 5][1:])
+        def last_of_unit(m):
+            return m[0] == "h" and m[2] == 3 and m[4] == HALF
+
+        for s in range(len(slots) + 7):
+            if s < len(slots):
+                for it in slots[s]:
+                    if it[0] == "h":
+                        h_mm(it[1], it[2], it[3], it[4])
+                    if it[0] == "q":
+                        f_qmm(it[1:])
+                    if it[0] == "f":
+                        f_mm(it[1:])
+            m1 = main(s - 1)
+            m2 = main(s - 2)
+            m3 = main(s - 3)
+            m4 = main(s - 4)
+            m5 = main(s - 5)
+            if m1[0] == "f":
+                f_res(m1[1:])
+            if m1[0] == "h" and m1[4] == HALF:
+                h_comp(m1[1], m1[2])
+            if last_of_unit(m2):
+                h_prod(m2[1], 0)
+            if m2[0] == "f":
+                f_cast(m2[1:])
+            if last_of_unit(m3):
+                h_prod(m3[1], 1)
+            if m3[0] == "f" and m3[3] % 2 == 1:
+                f_tr(m3[1:])
+            if m4[0] == "f" and m4[3] % 2 == 1:
+                f_evac(m4[1:])
+            m0 = main(s)
+            if m0[0] == "h":
+                for text in HOOKS.get((m0[1], m0[2], 1 if m0[3] else 0), []):
+                    hook(text)
+            if last_of_unit(m4):
+                h_q(m4[1])
+            if m5[0] == "f" and m5[3] % 2 == 1:
+                f_q(m5[1:])

@@ -20,30 +20,16 @@ HALF = 512
 HALVES = 2
 T4 = 4
 
-DVE_U = ((0, 1, 2, 3,), (0,), (0,), (0,), (0,), (0,), (0, 1, 2,), (0, 1, 2,))
-EVAC = {("z", 0, 0): "s", ("z", 0, 1): "s", ("x", 0, 0): "s", ("x", 0, 1): "v",
-        ("z", 1, 0): "s", ("z", 1, 1): "v", ("x", 1, 0): "s", ("x", 1, 1): "s"}
-FDVE = ((1,0,1), (1,1,1),)
-CAST_ACT = ((0,0,3), (0,1,1), (0,1,3), (1,0,1), (1,0,3), (1,1,1), (1,1,3),)
-EARLY_F = ((5,1), (5,2), (5,3),)
-EARLY_Q = ((4,2), (5,2), (6,2), (7,1), (7,3),)
-HOOKS = {
-    (0, 0, 0): ["w 1"],
-    (0, 0, 1): ["tr x 0 0"],
-    (0, 1, 1): ["ev x 0 0", "tr x 0 1"],
-    (0, 2, 1): ["ev x 0 1"],
-    (1, 1, 0): ["q x 0", "v 0", "tr z 1 0"],
-    (1, 2, 0): ["ev z 1 0", "tr z 1 1"],
-    (1, 3, 0): ["ev z 1 1"],
-    (2, 0, 0): ["lm 0"],
-    (2, 1, 0): ["q z 1", "tr x 1 0"],
-    (2, 2, 0): ["ev x 1 0", "tr x 1 1"],
-    (2, 3, 0): ["lq 0"],
-    (3, 0, 0): ["ev x 1 1"],
-    (3, 1, 0): ["q x 1"],
-    (3, 2, 0): ["lm 1"],
-    (3, 3, 0): ["lq 1"],
-}
+DVE_U = ((0, 1, 2, 3), (0,), (0,), (0,), (), (0,), (0, 1, 2), (0,))
+EVAC = {('z', 0, 0): 's', ('z', 0, 1): 's', ('x', 0, 0): 's', ('x', 0, 1): 'v', ('z', 1, 0): 's', ('z', 1, 1): 'v', ('x', 1, 0): 's', ('x', 1, 1): 's'}
+FDVE = ()
+CAST_ACT = ((0, 0, 1), (0, 0, 3), (0, 1, 1), (0, 1, 3), (1, 0, 1), (1, 0, 3), (1, 1, 1))
+EARLY_F = ((5, 2), (5, 3), (7, 0))
+EARLY_Q = ()
+LAG = {'hc': 1, 'hp0': 2, 'hp1': 3, 'hq': 4, 'fr': 1, 'fc': 2, 'ft': 4, 'fe': 5, 'fq': 6}
+BANKS = (3, 3)
+SWAP = (("z", 0), ("x", 0))
+HOOKS = {(0, 0, 0): ['sw x 0'], (0, 2, 0): ['w 1'], (0, 1, 1): ['tr x 0 0', 'ev x 0 0', 'tr x 0 1'], (0, 2, 1): ['ev x 0 1', 'v 0'], (1, 0, 0): ['q x 0'], (1, 1, 0): ['tr z 1 0', 'ev z 1 0'], (1, 2, 0): ['tr z 1 1', 'ev z 1 1', 'lm 0'], (3, 0, 0): ['q z 1', 'ev x 1 0'], (2, 2, 0): ['tr x 1 0', 'tr x 1 1'], (2, 3, 0): ['lq 0', 'ev x 1 1'], (4, 3, 0): ['q x 1'], (3, 1, 0): ['lm 1'], (3, 3, 0): ['lq 1']}
 
 
 def tile_crossheadtangentkernellinearisedlaplace_x2_kernel(
@@ -114,13 +100,26 @@ def tile_crossheadtangentkernellinearisedlaplace_x2_kernel(
         grouped = {}
         bank = {}
 
+        swapped = {}
+
+        def prep_swap(which, hf, b):
+            if (which, hf) in SWAP:
+                swapped[which, hf, b] = keep.tile([P, 2, 2, P], F32, align_bytes=64, name="swap_%s%d%d" % (which, hf, b))
+                nc.vector.tensor_copy(
+                    out=swapped[which, hf, b][:],
+                    in_=rows[which, hf][:, 2 * b : 2 * b + 2, :].bitcast(F32).rearrange("p j (q u) -> p j u q", u=2),
+                )
+
         def prep_tr(which, hf, b):
             t = psum.tile([P, 2, 2, P], F32, tag="tr", bufs=2, name="tr")
             bank[which, hf, b] = t
             for jj in range(2):
-                words = rows[which, hf][:, 2 * b + jj, :].bitcast(F32)
                 for u in range(2):
-                    nc.tensor.transpose(t[:, jj, u, :], words[:, u::2], ident[:])
+                    if (which, hf) in SWAP:
+                        s = swapped[which, hf, b][:, jj, u, :]
+                    else:
+                        s = rows[which, hf][:, 2 * b + jj, :].bitcast(F32)[:, u::2]
+                    nc.tensor.transpose(t[:, jj, u, :], s, ident[:])
 
         def prep_evac(which, hf, b, eng):
             if (which, hf) not in grouped:
@@ -197,7 +196,7 @@ def tile_crossheadtangentkernellinearisedlaplace_x2_kernel(
 
         def h_mm(k, t, c0, c1):
             which, hf, g = units[k]
-            acc = psum.tile([P, HALF], F32, tag="acc", bufs=4, name="acc")
+            acc = psum.tile([P, HALF], F32, tag="acc", bufs=BANKS[0], name="acc")
             if t == 0 and c0 == 0:
                 sig[k] = work.tile([P, T4, HALF], F32, align_bytes=64, name="sig")
                 comp[k] = work.tile([P, T4, HALF], F32, align_bytes=64, name="comp")
@@ -250,7 +249,7 @@ def tile_crossheadtangentkernellinearisedlaplace_x2_kernel(
         def f_qmm(f):
             hf, g, i = f
             cols = slice(P * i, P * (i + 1))
-            qa = psum.tile([P, HALF], F32, tag="acc", bufs=4, name="acc")
+            qa = psum.tile([P, HALF], F32, tag="acc", bufs=BANKS[0], name="acc")
             nc.tensor.matmul_mx(
                 out=qa[:],
                 lhsT=codes["l", hf][:, cols].bitcast(FP8X4),
@@ -260,13 +259,13 @@ def tile_crossheadtangentkernellinearisedlaplace_x2_kernel(
                 start=True,
                 stop=True,
             )
-            q_sb[f] = work.tile([P, HALF], F32, align_bytes=64, name="q_sb", bufs=12)
+            q_sb[f] = work.tile([P, HALF], F32, align_bytes=64, name="q_sb", bufs=16)
             nc.scalar.activation(q_sb[f][:], qa[:], ACT.Copy, scale=1.0 / math.sqrt(D), bias=1.0)
 
         def f_mm(f):
             hf, g, i = f
             cols = slice(P * i, P * (i + 1))
-            ta = psum.tile([P, HALF], F32, tag="tt", bufs=2, name="ta")
+            ta = psum.tile([P, HALF], F32, tag="tt", bufs=BANKS[1], name="ta")
             for kk in range(2):
                 nc.tensor.matmul_mx(
                     out=ta[:],
@@ -351,6 +350,9 @@ def tile_crossheadtangentkernellinearisedlaplace_x2_kernel(
         def hook(text):
             w = text.split(" ")
             a = [int(c) if c in ("0", "1") else c for c in w[1:]]
+            if w[0] == "sw":
+                prep_swap(a[0], a[1], 0)
+                prep_swap(a[0], a[1], 1)
             if w[0] == "tr":
                 prep_tr(a[0], a[1], a[2])
             if w[0] == "ev":
@@ -366,7 +368,9 @@ def tile_crossheadtangentkernellinearisedlaplace_x2_kernel(
             if w[0] == "v":
                 v_scale(a[0])
 
+        prep_swap("z", 0, 0)
         prep_tr("z", 0, 0)
+        prep_swap("z", 0, 1)
         prep_tr("z", 0, 1)
         w_perm(0)
         prep_evac("z", 0, 0, EVAC["z", 0, 0])
@@ -378,7 +382,7 @@ def tile_crossheadtangentkernellinearisedlaplace_x2_kernel(
         finals = [(hf, g, i) for hf in range(2) for g in range(2) for i in range(4)]
         items = []
         nf = 0
-        nq = 8
+        nq = 0
         for k in range(8):
             for part in range(2 if k == 0 else 1):
                 for t in range(T4):
@@ -387,14 +391,16 @@ def tile_crossheadtangentkernellinearisedlaplace_x2_kernel(
                     else:
                         items.append(("h", k, t, 0, HALF))
                     if (k, t) in EARLY_F:
-                        items.append(("q",) + finals[nf])
+                        if nq == nf:
+                            items.append(("q",) + finals[nf])
+                            nq += 1
                         items.append(("f",) + finals[nf])
                         nf += 1
                     if (k, t) in EARLY_Q:
                         items.append(("q",) + finals[nq])
                         nq += 1
         for n in range(nf, 16):
-            if n < 8 or n >= nq:
+            if n >= nq:
                 items.append(("q",) + finals[n])
             items.append(("f",) + finals[n])
 
@@ -415,7 +421,7 @@ def tile_crossheadtangentkernellinearisedlaplace_x2_kernel(
         def last_of_unit(m):
             return m[0] == "h" and m[2] == 3 and m[4] == HALF
 
-        for s in range(len(slots) + 7):
+        for s in range(len(slots) + 12):
             if s < len(slots):
                 for it in slots[s]:
                     if it[0] == "h":
@@ -424,30 +430,34 @@ def tile_crossheadtangentkernellinearisedlaplace_x2_kernel(
                         f_qmm(it[1:])
                     if it[0] == "f":
                         f_mm(it[1:])
-            m1 = main(s - 1)
-            m2 = main(s - 2)
-            m3 = main(s - 3)
-            m4 = main(s - 4)
-            m5 = main(s - 5)
-            if m1[0] == "f":
-                f_res(m1[1:])
-            if m1[0] == "h" and m1[4] == HALF:
-                h_comp(m1[1], m1[2])
-            if last_of_unit(m2):
-                h_prod(m2[1], 0)
-            if m2[0] == "f":
-                f_cast(m2[1:])
-            if last_of_unit(m3):
-                h_prod(m3[1], 1)
-            if m3[0] == "f" and m3[3] % 2 == 1:
-                f_tr(m3[1:])
-            if m4[0] == "f" and m4[3] % 2 == 1:
-                f_evac(m4[1:])
-            m0 = main(s)
-            if m0[0] == "h":
-                for text in HOOKS.get((m0[1], m0[2], 1 if m0[3] else 0), []):
+            m = main(s - LAG["fr"])
+            if m[0] == "f":
+                f_res(m[1:])
+            m = main(s - LAG["hc"])
+            if m[0] == "h" and m[4] == HALF:
+                h_comp(m[1], m[2])
+            m = main(s - LAG["hp0"])
+            if last_of_unit(m):
+                h_prod(m[1], 0)
+            m = main(s - LAG["fc"])
+            if m[0] == "f":
+                f_cast(m[1:])
+            m = main(s - LAG["hp1"])
+            if last_of_unit(m):
+                h_prod(m[1], 1)
+            m = main(s - LAG["ft"])
+            if m[0] == "f" and m[3] % 2 == 1:
+                f_tr(m[1:])
+            m = main(s - LAG["fe"])
+            if m[0] == "f" and m[3] % 2 == 1:
+                f_evac(m[1:])
+            m = main(s)
+            if m[0] == "h":
+                for text in HOOKS.get((m[1], m[2], 1 if m[3] else 0), []):
                     hook(text)
-            if last_of_unit(m4):
-                h_q(m4[1])
-            if m5[0] == "f" and m5[3] % 2 == 1:
-                f_q(m5[1:])
+            m = main(s - LAG["hq"])
+            if last_of_unit(m):
+                h_q(m[1])
+            m = main(s - LAG["fq"])
+            if m[0] == "f" and m[3] % 2 == 1:
+                f_q(m[1:])

import math
from contextlib import ExitStack

import concourse.mybir as mybir
from concourse.masks import make_identity

N, M, D, H = 1024, 1024, 512, 1024
FLOPS = 2 * (N * H * D + M * H * D + N * M * H + N * M * D)

F32 = mybir.dt.float32
BF16 = mybir.dt.bfloat16
I32 = mybir.dt.int32
U8 = mybir.dt.uint8
FP8X4 = mybir.dt.float8_e4m3fn_x4
ACT = mybir.ActivationFunctionType
ALU = mybir.AluOpType

P = 128
HALF = 512
HALVES = 2
T4 = 4

DVE_U = ((0, 1, 2, 3), (0,), (0,), (0,), (), (0,), (0, 1, 2), (0,))
EVAC = {('z', 0, 0): 's', ('z', 0, 1): 's', ('x', 0, 0): 's', ('x', 0, 1): 'v', ('z', 1, 0): 's', ('z', 1, 1): 'v', ('x', 1, 0): 's', ('x', 1, 1): 's'}
FDVE = ()
CAST_ACT = ((0, 0, 1), (0, 0, 3), (0, 1, 1), (0, 1, 3), (1, 0, 1), (1, 0, 3), (1, 1, 1))
EARLY_F = ((5, 2), (5, 3), (7, 0))
EARLY_Q = ()
LAG = {'hc': 1, 'hp0': 2, 'hp1': 3, 'hq': 4, 'fr': 1, 'fc': 2, 'ft': 4, 'fe': 5, 'fq': 6}
BANKS = (3, 3)
SWAP = (("z", 0), ("x", 0))
HOOKS = {(0, 0, 0): ['sw x 0'], (0, 2, 0): ['w 1'], (0, 1, 1): ['tr x 0 0', 'ev x 0 0', 'tr x 0 1'], (0, 2, 1): ['ev x 0 1', 'v 0'], (1, 0, 0): ['q x 0'], (1, 1, 0): ['tr z 1 0', 'ev z 1 0'], (1, 2, 0): ['tr z 1 1', 'ev z 1 1', 'lm 0'], (3, 0, 0): ['q z 1', 'ev x 1 0'], (2, 2, 0): ['tr x 1 0', 'tr x 1 1'], (2, 3, 0): ['lq 0', 'ev x 1 1'], (4, 3, 0): ['q x 1'], (3, 1, 0): ['lm 1'], (3, 3, 0): ['lq 1']}


def tile_crossheadtangentkernellinearisedlaplace_x2_kernel(
    tc, x, z, w_words, w_scales, lam, v1, v2, out_0, out_1, out_2
):
    nc = tc.nc
    with ExitStack() as ctx:
        keep = ctx.enter_context(tc.tile_pool(name="keep", bufs=1))
        work = ctx.enter_context(tc.tile_pool(name="work", bufs=3))
        psum = ctx.enter_context(tc.psum_pool(name="psum", bufs=2))
        ctx.enter_context(tc.manual_schedule())

        warm = keep.tile([P, 1], F32, name="warm")
        nc.vector.memset(warm[:], 0.0)
        warm_out = keep.tile([P, 1], F32, name="warm_out")
        nc.scalar.activation(warm_out[:], warm[:], ACT.Sigmoid)
        ws_raw = keep.tile([P, H], U8, align_bytes=64, name="ws_raw")
        nc.vector.memset(ws_raw[:].bitcast(I32), 0)
        v_raw = [keep.tile([P, 2, T4], BF16, name="v_raw%d" % o) for o in range(2)]
        lam_sb = keep.tile([P, T4], BF16, name="lam_sb")
        ident = keep.tile([P, P], F32, name="ident")
        make_identity(nc, ident[:])

        rows = {}
        src = {"x": x, "z": z}

        def load_rows(which, hf, j0, nj):
            if (which, hf) not in rows:
                rows[which, hf] = keep.tile([P, 4, D], BF16, align_bytes=64, name="rows_%s%d" % (which, hf))
            nc.sync.dma_start(
                out=rows[which, hf][:, j0 : j0 + nj, :],
                in_=src[which][HALF * hf + P * j0 : HALF * hf + P * (j0 + nj), :].rearrange("(j p) k -> p j k", p=P),
            )

        load_rows("z", 0, 0, 2)
        w_raw = keep.tile([P, H], I32, align_bytes=64, name="w_raw")
        w_dram = w_words[0].rearrange("p n t -> p (n t)")

        def load_w(g):
            nc.sync.dma_start(
                out=w_raw[:, HALF * g : HALF * (g + 1)],
                in_=w_dram[:, 4 * HALF * g : 4 * HALF * (g + 1)].bitcast(I32),
            )

        for q in range(4):
            nc.sync.dma_start(
                out=ws_raw[32 * q : 32 * q + 4, :].bitcast(I32),
                in_=w_scales[0, 4 * q : 4 * q + 4, :].bitcast(I32),
            )
        load_w(0)
        load_rows("z", 0, 2, 2)
        nc.sync.dma_start(out=v_raw[1][:], in_=v2.rearrange("(g p t) -> p g t", p=P, t=T4))
        load_w(1)
        load_rows("x", 0, 0, 4)
        nc.sync.dma_start(out=v_raw[0][:], in_=v1.rearrange("(g p t) -> p g t", p=P, t=T4))
        nc.sync.dma_start(out=lam_sb[:], in_=lam.rearrange("(p t) -> p t", t=T4))
        load_rows("z", 1, 0, 4)
        load_rows("x", 1, 0, 4)


        v_pos = keep.tile([P, 2, 2, T4], F32, name="v_pos")
        v_neg = keep.tile([P, 2, 2, T4], F32, name="v_neg")

        def v_scale(o):
            nc.vector.tensor_scalar(out=v_pos[:, o], in0=v_raw[o][:], scalar1=4.0, scalar2=None, op0=ALU.mult)
            nc.vector.tensor_scalar(out=v_neg[:, o], in0=v_raw[o][:], scalar1=-4.0, scalar2=None, op0=ALU.mult)

        grouped = {}
        bank = {}

        swapped = {}

        def prep_swap(which, hf, b):
            if (which, hf) in SWAP:
                swapped[which, hf, b] = keep.tile([P, 2, 2, P], F32, align_bytes=64, name="swap_%s%d%d" % (which, hf, b))
                nc.vector.tensor_copy(
                    out=swapped[which, hf, b][:],
                    in_=rows[which, hf][:, 2 * b : 2 * b + 2, :].bitcast(F32).rearrange("p j (q u) -> p j u q", u=2),
                )

        def prep_tr(which, hf, b):
            t = psum.tile([P, 2, 2, P], F32, tag="tr", bufs=2, name="tr")
            bank[which, hf, b] = t
            for jj in range(2):
                for u in range(2):
                    if (which, hf) in SWAP:
                        s = swapped[which, hf, b][:, jj, u, :]
                    else:
                        s = rows[which, hf][:, 2 * b + jj, :].bitcast(F32)[:, u::2]
                    nc.tensor.transpose(t[:, jj, u, :], s, ident[:])

        def prep_evac(which, hf, b, eng):
            if (which, hf) not in grouped:
                grouped[which, hf] = keep.tile([P, HALF, T4], BF16, align_bytes=64, name="grouped_%s%d" % (which, hf))
            dst = (
                grouped[which, hf][:, 256 * b : 256 * (b + 1), :]
                .rearrange("p n t -> p (n t)")
                .bitcast(F32)
                .rearrange("p (j r u) -> p j r u", j=2, u=2)
            )
            s = bank[which, hf, b][:].rearrange("p j u r -> p j r u")
            if eng == "v":
                nc.vector.tensor_copy(out=dst, in_=s)
            else:
                nc.scalar.copy(out=dst, in_=s)

        codes = {}
        scales = {}

        def quantize(key, tile3, pool=keep):
            name = "_".join(str(k) for k in key)
            codes[key] = pool.tile([P, HALF], I32, align_bytes=64, name="codes_" + name)
            scales[key] = pool.tile([P, HALF], U8, align_bytes=64, name="scales_" + name)
            nc.vector.quantize_mx(
                out=codes[key][:].bitcast(FP8X4),
                scales=scales[key][:],
                in_=tile3[:].rearrange("p n t -> p (n t)"),
            )

        def prep_q(which, hf, b=None):
            if b is None:
                quantize((which, hf), grouped[which, hf])
                return
            key = (which, hf)
            if b == 0:
                codes[key] = keep.tile([P, HALF], I32, align_bytes=64, name="codes_%s%d" % key)
                scales[key] = keep.tile([P, HALF], U8, align_bytes=64, name="scales_%s%d" % key)
            cols = slice(256 * b, 256 * (b + 1))
            nc.vector.quantize_mx(
                out=codes[key][:, cols].bitcast(FP8X4),
                scales=scales[key][:, cols],
                in_=grouped[key][:, cols, :].rearrange("p n t -> p (n t)"),
            )

        xl = {}

        def lam_mul(hf):
            xl[hf] = keep.tile([P, HALF, T4], BF16, align_bytes=64, name="xl%d" % hf)
            nc.vector.tensor_tensor(
                out=xl[hf][:],
                in0=grouped["x", hf][:],
                in1=lam_sb[:].unsqueeze(1).to_broadcast([P, HALF, T4]),
                op=ALU.mult,
            )

        def lam_q(hf):
            quantize(("l", hf), xl[hf])

        w_codes = keep.tile([P, H], I32, align_bytes=64, name="w_codes")
        w_sc = keep.tile([P, H], U8, align_bytes=64, name="w_sc")

        def w_perm(g):
            cols = slice(HALF * g, HALF * (g + 1))
            for dst, s in ((w_codes, w_raw), (w_sc, ws_raw)):
                nc.vector.tensor_copy(
                    out=dst[:, cols].rearrange("p (t m) -> p t m", t=T4),
                    in_=s[:, cols].rearrange("p (m t) -> p t m", t=T4),
                )

        units = [("z", 0, 0), ("z", 0, 1), ("x", 0, 0), ("x", 0, 1), ("z", 1, 0), ("z", 1, 1), ("x", 1, 0), ("x", 1, 1)]
        sig = {}
        comp = {}
        abf = {}

        def h_mm(k, t, c0, c1):
            which, hf, g = units[k]
            acc = psum.tile([P, HALF], F32, tag="acc", bufs=BANKS[0], name="acc")
            if t == 0 and c0 == 0:
                sig[k] = work.tile([P, T4, HALF], F32, align_bytes=64, name="sig")
                comp[k] = work.tile([P, T4, HALF], F32, align_bytes=64, name="comp")
            h0 = HALF * g + P * t
            nc.tensor.matmul_mx(
                out=acc[:, : c1 - c0],
                lhsT=w_codes[:, h0 : h0 + P].bitcast(FP8X4),
                lhsT_scale=w_sc[:, h0 : h0 + P],
                rhs=codes[which, hf][:, c0:c1].bitcast(FP8X4),
                rhs_scale=scales[which, hf][:, c0:c1],
                start=True,
                stop=True,
            )
            nc.scalar.activation(sig[k][:, t, c0:c1], acc[:, : c1 - c0], ACT.Sigmoid, scale=2.0)

        def h_comp(k, t):
            which, hf, g = units[k]
            o = 0 if which == "x" else 1
            neg = v_neg[:, o, g, t : t + 1]
            pos = v_pos[:, o, g, t : t + 1]
            if t in DVE_U[k]:
                nc.vector.tensor_scalar(
                    out=comp[k][:, t, :], in0=sig[k][:, t, :], scalar1=neg, scalar2=pos, op0=ALU.mult, op1=ALU.add
                )
            else:
                nc.scalar.activation(comp[k][:, t, :], sig[k][:, t, :], ACT.Identity, bias=pos, scale=neg)

        def h_prod(k, part):
            if part == 0:
                abf[k] = work.tile([P, HALF, T4], BF16, align_bytes=64, name="abf")
            cols = slice(256 * part, 256 * (part + 1))
            nc.vector.tensor_tensor(
                out=abf[k][:, cols, :].rearrange("p (c i) t -> p c t i", i=4),
                in0=sig[k][:, :, cols].rearrange("p t (c i) -> p c t i", i=4),
                in1=comp[k][:, :, cols].rearrange("p t (c i) -> p c t i", i=4),
                op=ALU.mult,
            )

        def h_q(k):
            which, hf, g = units[k]
            quantize(("h" + which, hf, g), abf[k])

        q_sb = {}
        t_ps = {}
        res = {}
        res16 = {}
        pbank = {}
        pgr = {}

        def f_qmm(f):
            hf, g, i = f
            cols = slice(P * i, P * (i + 1))
            qa = psum.tile([P, HALF], F32, tag="acc", bufs=BANKS[0], name="acc")
            nc.tensor.matmul_mx(
                out=qa[:],
                lhsT=codes["l", hf][:, cols].bitcast(FP8X4),
                lhsT_scale=scales["l", hf][:, cols],
                rhs=codes["z", g][:].bitcast(FP8X4),
                rhs_scale=scales["z", g][:],
                start=True,
                stop=True,
            )
            q_sb[f] = work.tile([P, HALF], F32, align_bytes=64, name="q_sb", bufs=16)
            nc.scalar.activation(q_sb[f][:], qa[:], ACT.Copy, scale=1.0 / math.sqrt(D), bias=1.0)

        def f_mm(f):
            hf, g, i = f
            cols = slice(P * i, P * (i + 1))
            ta = psum.tile([P, HALF], F32, tag="tt", bufs=BANKS[1], name="ta")
            for kk in range(2):
                nc.tensor.matmul_mx(
                    out=ta[:],
                    lhsT=codes["hx", hf, kk][:, cols].bitcast(FP8X4),
                    lhsT_scale=scales["hx", hf, kk][:, cols],
                    rhs=codes["hz", g, kk][:].bitcast(FP8X4),
                    rhs_scale=scales["hz", g, kk][:],
                    start=(kk == 0),
                    stop=(kk == 1),
                )
            t_ps[f] = ta

        def f_res(f):
            hf, g, i = f
            res[f] = work.tile([P, HALF], F32, align_bytes=64, name="res", bufs=4)
            nc.vector.scalar_tensor_tensor(
                out=res[f][:], in0=t_ps[f][:], scalar=1.0 / math.sqrt(H), in1=q_sb[f][:], op0=ALU.mult, op1=ALU.mult
            )
            r0 = HALF * hf + P * i
            nc.sync.dma_start(out=out_0[r0 : r0 + P, HALF * g : HALF * (g + 1)], in_=res[f][:])

        def f_cast(f):
            res16[f] = work.tile([P, HALF], BF16, align_bytes=64, name="res16", bufs=4)
            dst = res16[f][:].rearrange("p (u q e) -> p u q e", u=2, e=2)
            s = res[f][:].rearrange("p (q u e) -> p u q e", u=2, e=2)
            if f in CAST_ACT:
                nc.scalar.copy(out=dst, in_=s)
            else:
                nc.vector.tensor_copy(out=dst, in_=s)

        def f_tr(f):
            hf, g, i = f
            bk = psum.tile([P, 2, 2, P], F32, tag="tr", bufs=2, name="tr")
            pbank[hf, g, i // 2] = bk
            for jj in range(2):
                words = res16[hf, g, i - 1 + jj][:].bitcast(F32)
                for u in range(2):
                    nc.tensor.transpose(bk[:, jj, u, :], words[:, P * u : P * (u + 1)], ident[:])

        def f_evac(f):
            hf, g, i = f
            b = i // 2
            if b == 0:
                pgr[hf, g] = work.tile([P, HALF, T4], BF16, align_bytes=64, name="pgr", bufs=2)
            dst = (
                pgr[hf, g][:, 256 * b : 256 * (b + 1), :]
                .rearrange("p n t -> p (n t)")
                .bitcast(F32)
                .rearrange("p (j r u) -> p j r u", j=2, u=2)
            )
            s = pbank[hf, g, b][:].rearrange("p j u r -> p j r u")
            if f in FDVE:
                nc.vector.tensor_copy(out=dst, in_=s)
            else:
                nc.scalar.copy(out=dst, in_=s)

        def f_q(f):
            hf, g, i = f
            b = i // 2
            key = ("p", hf, g)
            if b == 0:
                codes[key] = keep.tile([P, HALF], I32, align_bytes=64, name="codes_p%d%d" % (hf, g))
                scales[key] = keep.tile([P, HALF], U8, align_bytes=64, name="scales_p%d%d" % (hf, g))
            cols = slice(256 * b, 256 * (b + 1))
            nc.vector.quantize_mx(
                out=codes[key][:, cols].bitcast(FP8X4),
                scales=scales[key][:, cols],
                in_=pgr[hf, g][:, cols, :].rearrange("p n t -> p (n t)"),
            )
            c0 = HALF * hf + 256 * b
            nc.sync.dma_start(
                out=out_1[g].rearrange("p n t -> p (n t)")[:, 4 * c0 : 4 * (c0 + 256)].bitcast(I32),
                in_=codes[key][:, cols],
            )
            if b == 1:
                for q in range(4):
                    nc.sync.dma_start(
                        out=out_2[g, 4 * q : 4 * q + 4, HALF * hf : HALF * (hf + 1)].bitcast(I32),
                        in_=scales[key][32 * q : 32 * q + 4, :].bitcast(I32),
                    )

        def hook(text):
            w = text.split(" ")
            a = [int(c) if c in ("0", "1") else c for c in w[1:]]
            if w[0] == "sw":
                prep_swap(a[0], a[1], 0)
                prep_swap(a[0], a[1], 1)
            if w[0] == "tr":
                prep_tr(a[0], a[1], a[2])
            if w[0] == "ev":
                prep_evac(a[0], a[1], a[2], EVAC[a[0], a[1], a[2]])
            if w[0] == "q":
                prep_q(a[0], a[1])
            if w[0] == "lm":
                lam_mul(a[0])
            if w[0] == "lq":
                lam_q(a[0])
            if w[0] == "w":
                w_perm(a[0])
            if w[0] == "v":
                v_scale(a[0])

        prep_swap("z", 0, 0)
        prep_tr("z", 0, 0)
        prep_swap("z", 0, 1)
        prep_tr("z", 0, 1)
        w_perm(0)
        prep_evac("z", 0, 0, EVAC["z", 0, 0])
        prep_q("z", 0, 0)
        prep_evac("z", 0, 1, EVAC["z", 0, 1])
        prep_q("z", 0, 1)
        v_scale(1)

        finals = [(hf, g, i) for hf in range(2) for g in range(2) for i in range(4)]
        items = []
        nf = 0
        nq = 0
        for k in range(8):
            for part in range(2 if k == 0 else 1):
                for t in range(T4):
                    if k == 0:
                        items.append(("h", k, t, 256 * part, 256 * (part + 1)))
                    else:
                        items.append(("h", k, t, 0, HALF))
                    if (k, t) in EARLY_F:
                        if nq == nf:
                            items.append(("q",) + finals[nf])
                            nq += 1
                        items.append(("f",) + finals[nf])
                        nf += 1
                    if (k, t) in EARLY_Q:
                        items.append(("q",) + finals[nq])
                        nq += 1
        for n in range(nf, 16):
            if n >= nq:
                items.append(("q",) + finals[n])
            items.append(("f",) + finals[n])

        slots = []
        cur = []
        for it in items:
            cur.append(it)
            if it[0] != "q":
                slots.append(cur)
                cur = []
        assert not cur

        def main(s):
            if 0 <= s < len(slots):
                return slots[s][-1]
            return ("none",)

        def last_of_unit(m):
            return m[0] == "h" and m[2] == 3 and m[4] == HALF

        for s in range(len(slots) + 12):
            if s < len(slots):
                for it in slots[s]:
                    if it[0] == "h":
                        h_mm(it[1], it[2], it[3], it[4])
                    if it[0] == "q":
                        f_qmm(it[1:])
                    if it[0] == "f":
                        f_mm(it[1:])
            m = main(s - LAG["fr"])
            if m[0] == "f":
                f_res(m[1:])
            m = main(s - LAG["hc"])
            if m[0] == "h" and m[4] == HALF:
                h_comp(m[1], m[2])
            m = main(s - LAG["hp0"])
            if last_of_unit(m):
                h_prod(m[1], 0)
            m = main(s - LAG["fc"])
            if m[0] == "f":
                f_cast(m[1:])
            m = main(s - LAG["hp1"])
            if last_of_unit(m):
                h_prod(m[1], 1)
            m = main(s - LAG["ft"])
            if m[0] == "f" and m[3] % 2 == 1:
                f_tr(m[1:])
            m = main(s - LAG["fe"])
            if m[0] == "f" and m[3] % 2 == 1:
                f_evac(m[1:])
            m = main(s)
            if m[0] == "h":
                for text in HOOKS.get((m[1], m[2], 1 if m[3] else 0), []):
                    hook(text)
            m = main(s - LAG["hq"])
            if last_of_unit(m):
                h_q(m[1])
            m = main(s - LAG["fq"])
            if m[0] == "f" and m[3] % 2 == 1:
                f_q(m[1:])
